import numpy as np
import ml_dtypes


def mxq(x, axis, fmt="e4m3"):
    dtype, down = {"e4m3": (ml_dtypes.float8_e4m3fn, 7), "e5m2": (ml_dtypes.float8_e5m2, 14)}[fmt]
    v = np.moveaxis(np.asarray(x, np.float32).astype(ml_dtypes.bfloat16).astype(np.float64), axis, -1)
    blocks = v.reshape(v.shape[:-1] + (-1, 32))
    amax = np.abs(blocks).max(-1, keepdims=True)
    byte = np.maximum(np.where(amax > 0, np.frexp(amax)[1] - 1 + 127, 0) - down, 1)
    scale = np.exp2(byte - 127.0)
    codes = (blocks / scale).astype(np.float32).astype(dtype).astype(np.float64)
    return np.moveaxis((codes * scale).reshape(v.shape), -1, axis)


WIDE = False


def mx_kscale(k):
    if not WIDE:
        return np.ones(k)
    levels = np.array([10, -10, 5, -5, 0])
    if k % 512:
        return np.exp2(np.random.permutation(np.resize(levels, k // 32))).repeat(32)
    a = np.empty((k // 512, 16))
    for p in range(k // 512):
        a[p, :8] = np.random.permutation(np.resize(levels, 8))
        for g in range(8):
            far = levels[np.abs(levels - a[p, g]) >= 10]
            a[p, g + 8] = far[np.random.randint(len(far))]
    return np.exp2(a.ravel()).repeat(32)


def f64(x):
    return np.asarray(x).astype(np.float64)


def striped(idx):
    return np.tile(idx.reshape(-1, 16).T, (8, 1)).astype(np.uint16)


def unstriped(offs):
    return offs[:16].T.reshape(-1).astype(np.int64)


def pack_weight(w):
    k, n = w.shape
    w = f64(np.asarray(w, np.float32).astype(ml_dtypes.bfloat16)).reshape(k // 32, 32, n)
    amax = np.abs(w).max(1)
    byte = np.clip(np.where(amax > 0, np.frexp(amax)[1] - 1 + 127 - 7, 1), 1, 254)
    scaled = (w * np.exp2(127.0 - byte)[:, None, :]).reshape(k, n).astype(np.float32)
    words = np.ascontiguousarray(scaled.reshape(k // 512, 128, 4, n).transpose(0, 1, 3, 2)).astype(ml_dtypes.float8_e4m3fn).view(np.uint8)
    return words, np.ascontiguousarray(byte.astype(np.uint8).reshape(k // 512, 16, n))


def unpack_weight(words, scales):
    g, p, n, _ = words.shape
    vals = np.ascontiguousarray(words).view(ml_dtypes.float8_e4m3fn).astype(np.float64) * np.repeat(np.exp2(scales.astype(np.float64) - 127.0), 8, axis=1)[..., None]
    return vals.transpose(0, 1, 3, 2).reshape(g * 512, n)


K, T, S, N = 1024, 2048, 1024, 512


def setup_inputs():
    n = np.random.standard_normal
    s = mx_kscale(K)[:, None]
    w1, w2 = n((2, K, N)) / np.sqrt(2 * K) / s[None]
    packed = pack_weight(n((K, T)) * s)
    return {
        "xT": (n((K, S)) * s).astype(np.float32),
        "s_words": packed[0],
        "s_scales": packed[1],
        "w1": w1.astype(np.float32),
        "w2": w2.astype(np.float32),
        "b": (0.3 * n((N, 1))).astype(np.float32),
        "offs": striped(np.random.permutation(T)[:S]),
    }


def reference(xT, s_words, s_scales, w1, w2, b, offs):
    y = mxq(f64(w1), 0, "e4m3").T @ mxq(f64(xT), 0, "e4m3") + mxq(f64(w2), 0, "e4m3").T @ unpack_weight(s_words, s_scales)[:, unstriped(offs)]
    return y + f64(b)

@@ -1,0 +1,189 @@
+from contextlib import ExitStack
+
+import concourse.mybir as mybir
+
+K, T, S, N = 1024, 2048, 1024, 512
+FLOPS = 2 * 2 * K * N * S
+
+F32 = mybir.dt.float32
+BF16 = mybir.dt.bfloat16
+I32 = mybir.dt.int32
+U32 = mybir.dt.uint32
+U16 = mybir.dt.uint16
+U8 = mybir.dt.uint8
+FP8X4 = mybir.dt.float8_e4m3fn_x4
+IDENTITY = mybir.ActivationFunctionType.Identity
+
+P = 128
+PACK = 4
+K_PASS = P * PACK
+PASSES = K // K_PASS
+M_TILES = N // P
+QUADRANT = 32
+SCALE_ROWS = 4
+
+
+def tile_picked_recall_bias_p_kernel(tc, xT, s_words, s_scales, w1, w2, b, offs, out):
+    nc = tc.nc
+
+    with ExitStack() as ctx:
+        keep = ctx.enter_context(tc.tile_pool(name="keep", bufs=1))
+        psum = ctx.enter_context(tc.psum_pool(name="psum", bufs=1))
+
+        offsets = keep.tile([P, S // 16], U16, name="offsets")
+        store_scales = keep.tile([P, T], U8, name="store_scales", align_bytes=64)
+        nc.vector.memset(store_scales[:].bitcast(I32), 0)
+        for q in range(P // QUADRANT):
+            nc.scalar.dma_start(
+                out=store_scales[QUADRANT * q : QUADRANT * q + PASSES * SCALE_ROWS, :].bitcast(I32),
+                in_=s_scales[:, SCALE_ROWS * q : SCALE_ROWS * (q + 1), :].bitcast(I32),
+            )
+        bias = keep.tile([P, M_TILES, 1], F32, name="bias")
+        with nc.allow_non_contiguous_dma(reason="one bias value for each partition and row tile"):
+            nc.scalar.dma_start(out=bias[:], in_=b.rearrange("(t p) o -> p t o", p=P))
+
+        def load_words(g):
+            window = keep.tile([P, T], I32, name="store_words%d" % g, align_bytes=64)
+            nc.sync.dma_start(out=window[:], in_=s_words[g].rearrange("p c r -> p (c r)").bitcast(I32))
+            return window
+
+        def load_rows(name, matrix, g, cols):
+            width = cols.stop - cols.start
+            raw = keep.tile([P, PACK, width], F32, name=name + "_raw")
+            rows = matrix[g * K_PASS : (g + 1) * K_PASS, cols]
+            nc.sync.dma_start(out=raw[:], in_=rows.rearrange("(p j) w -> p j w", j=PACK))
+            return raw
+
+        def interleave(name, raw, vector_cols):
+            width = raw.shape[2]
+            grouped = keep.tile([P, width, PACK], BF16, name=name + "_bf16", align_bytes=64)
+            split = width - vector_cols
+            if split > 0:
+                nc.scalar.copy(
+                    out=grouped[:, :split, :].rearrange("p (c i) j -> p c j i", i=4),
+                    in_=raw[:, :, :split].rearrange("p j (c i) -> p c j i", i=4),
+                )
+            if vector_cols > 0:
+                nc.vector.tensor_copy(
+                    out=grouped[:, split:, :].rearrange("p (c i) j -> p c j i", i=4),
+                    in_=raw[:, :, split:].rearrange("p j (c i) -> p c j i", i=4),
+                )
+            return grouped
+
+        def quantize(name, grouped):
+            width = grouped.shape[1]
+            codes = keep.tile([P, width], U32, name=name + "_codes", align_bytes=64)
+            scales = keep.tile([P, width], U8, name=name + "_scales", align_bytes=64)
+            nc.vector.quantize_mx(
+                out=codes[:].bitcast(FP8X4), scales=scales[:], in_=grouped[:].rearrange("p w j -> p (w j)")
+            )
+            return codes, scales
+
+        def gather_words(g, window):
+            picked = keep.tile([P, S], U32, name="picked_words%d" % g, align_bytes=64)
+            nc.vector.tensor_copy(out=picked[:], in_=window[:].bitcast(U32).indirect(offsets[:]))
+            return picked
+
+        def one_pass(banks, weights, codes, scales, start, stop):
+            w_codes, w_scales = weights
+            for t in range(M_TILES):
+                m = slice(t * P, (t + 1) * P)
+                nc.tensor.matmul_mx(
+                    out=banks[t][:],
+                    lhsT=w_codes[:, m].bitcast(FP8X4),
+                    lhsT_scale=w_scales[:, m],
+                    rhs=codes.bitcast(FP8X4),
+                    rhs_scale=scales,
+                    start=start,
+                    stop=stop,
+                )
+
+        def open_banks(first, width):
+            return [psum.tile([P, width], F32, name="bank%d" % (first + t), tag="bank%d" % (first + t)) for t in range(M_TILES)]
+
+        out_rows = out.rearrange("(t p) c -> p t c", p=P)
+
+        def finish(name, banks, cols, vector_tiles, tiles_per_store):
+            width = cols.stop - cols.start
+            result = keep.tile([P, M_TILES, width], F32, name=name + "_result")
+            for t in range(M_TILES):
+                if t in vector_tiles:
+                    nc.vector.tensor_scalar_add(result[:, t, :], banks[t][:], bias[:, t, :])
+                else:
+                    nc.scalar.activation(out=result[:, t, :], in_=banks[t][:], func=IDENTITY, bias=bias[:, t, :])
+                if (t + 1) % tiles_per_store == 0:
+                    ts = slice(t + 1 - tiles_per_store, t + 1)
+                    nc.sync.dma_start(out=out_rows[:, ts, cols], in_=result[:, ts, :])
+
+        all_m = slice(0, N)
+        c0 = slice(0, 256)
+        c1 = slice(256, 512)
+        c2 = slice(512, 768)
+        c3 = slice(768, 1024)
+
+        words0 = load_words(0)
+        nc.sync.dma_start(out=offsets[:], in_=offs)
+        w2_raw0 = load_rows("w2_0", w2, 0, all_m)
+        words1 = load_words(1)
+        w2_raw1 = load_rows("w2_1", w2, 1, all_m)
+        w1_raw0 = load_rows("w1_0", w1, 0, all_m)
+        x0_raw0 = load_rows("x0_0", xT, 0, c0)
+        w1_raw1 = load_rows("w1_1", w1, 1, all_m)
+        x0_raw1 = load_rows("x0_1", xT, 1, c0)
+        x1_raw0 = load_rows("x1_0", xT, 0, c1)
+        x1_raw1 = load_rows("x1_1", xT, 1, c1)
+        x2_raw0 = load_rows("x2_0", xT, 0, c2)
+        x2_raw1 = load_rows("x2_1", xT, 1, c2)
+        x3_raw0 = load_rows("x3_0", xT, 0, c3)
+        x3_raw1 = load_rows("x3_1", xT, 1, c3)
+
+        picked0 = gather_words(0, words0)
+        w2_bf0 = interleave("w2_0", w2_raw0, 0)
+        picked_scales = keep.tile([P, S], U8, name="picked_scales", align_bytes=64)
+        nc.vector.tensor_copy(out=picked_scales[:], in_=store_scales[:].indirect(offsets[:]))
+        w2_q0 = quantize("w2_0", w2_bf0)
+        picked1 = gather_words(1, words1)
+
+        banks0 = open_banks(0, 256)
+        banks1 = open_banks(M_TILES, 256)
+        one_pass(banks0, w2_q0, picked0[:, c0], picked_scales[:, c0], True, False)
+        one_pass(banks1, w2_q0, picked0[:, c1], picked_scales[:, c1], True, False)
+        w2_q1 = quantize("w2_1", interleave("w2_1", w2_raw1, 128))
+        one_pass(banks0, w2_q1, picked1[:, c0], picked_scales[SCALE_ROWS:, c0], False, False)
+        one_pass(banks1, w2_q1, picked1[:, c1], picked_scales[SCALE_ROWS:, c1], False, False)
+        w1_q0 = quantize("w1_0", interleave("w1_0", w1_raw0, 256))
+
+        x_bf = interleave("x0_0", x0_raw0, 128)
+        x_codes0, x_scales0 = quantize("x0_0", x_bf)
+        w1_q1 = quantize("w1_1", interleave("w1_1", w1_raw1, 256))
+        one_pass(banks0, w1_q0, x_codes0[:], x_scales0[:], False, False)
+        x_codes1, x_scales1 = quantize("x0_1", interleave("x0_1", x0_raw1, 160))
+        one_pass(banks0, w1_q1, x_codes1[:], x_scales1[:], False, True)
+
+        x_bf = interleave("x1_0", x1_raw0, 192)
+        finish("c0", banks0, c0, (), 4)
+        x_codes0, x_scales0 = quantize("x1_0", x_bf)
+        one_pass(banks1, w1_q0, x_codes0[:], x_scales0[:], False, False)
+        x_codes1, x_scales1 = quantize("x1_1", interleave("x1_1", x1_raw1, 192))
+        one_pass(banks1, w1_q1, x_codes1[:], x_scales1[:], False, True)
+        banks2 = open_banks(0, 256)
+        one_pass(banks2, w2_q0, picked0[:, c2], picked_scales[:, c2], True, False)
+        one_pass(banks2, w2_q1, picked1[:, c2], picked_scales[SCALE_ROWS:, c2], False, False)
+
+        x_bf = interleave("x2_0", x2_raw0, 192)
+        finish("c1", banks1, c1, (), 4)
+        x_codes0, x_scales0 = quantize("x2_0", x_bf)
+        one_pass(banks2, w1_q0, x_codes0[:], x_scales0[:], False, False)
+        x_codes1, x_scales1 = quantize("x2_1", interleave("x2_1", x2_raw1, 192))
+        one_pass(banks2, w1_q1, x_codes1[:], x_scales1[:], False, True)
+        banks3 = open_banks(4, 256)
+        one_pass(banks3, w2_q0, picked0[:, c3], picked_scales[:, c3], True, False)
+        one_pass(banks3, w2_q1, picked1[:, c3], picked_scales[SCALE_ROWS:, c3], False, False)
+
+        x_bf = interleave("x3_0", x3_raw0, 192)
+        finish("c2", banks2, c2, (), 4)
+        x_codes0, x_scales0 = quantize("x3_0", x_bf)
+        one_pass(banks3, w1_q0, x_codes0[:], x_scales0[:], False, False)
+        x_codes1, x_scales1 = quantize("x3_1", interleave("x3_1", x3_raw1, 168))
+        one_pass(banks3, w1_q1, x_codes1[:], x_scales1[:], False, True)
+        finish("c3", banks3, c3, (1, 3,), 2)

@@ -1,6 +1,7 @@
 from contextlib import ExitStack
 
 import concourse.mybir as mybir
+from concourse.masks import make_identity
 
 K, T, S, N = 1024, 2048, 1024, 512
 FLOPS = 2 * 2 * K * N * S
@@ -28,9 +29,11 @@ def tile_picked_recall_bias_p_kernel(tc, xT, s_words, s_scales, w1, w2, b, offs,
 
     with ExitStack() as ctx:
         keep = ctx.enter_context(tc.tile_pool(name="keep", bufs=1))
+        stage = ctx.enter_context(tc.tile_pool(name="stage", bufs=3))
         psum = ctx.enter_context(tc.psum_pool(name="psum", bufs=1))
 
         offsets = keep.tile([P, S // 16], U16, name="offsets")
+        nc.sync.dma_start(out=offsets[:], in_=offs)
         store_scales = keep.tile([P, T], U8, name="store_scales", align_bytes=64)
         nc.vector.memset(store_scales[:].bitcast(I32), 0)
         for q in range(P // QUADRANT):
@@ -38,20 +41,28 @@ def tile_picked_recall_bias_p_kernel(tc, xT, s_words, s_scales, w1, w2, b, offs,
                 out=store_scales[QUADRANT * q : QUADRANT * q + PASSES * SCALE_ROWS, :].bitcast(I32),
                 in_=s_scales[:, SCALE_ROWS * q : SCALE_ROWS * (q + 1), :].bitcast(I32),
             )
-        bias = keep.tile([P, M_TILES, 1], F32, name="bias")
-        with nc.allow_non_contiguous_dma(reason="one bias value for each partition and row tile"):
-            nc.scalar.dma_start(out=bias[:], in_=b.rearrange("(t p) o -> p t o", p=P))
+
+        bias_rows = keep.tile([P, P], F32, name="bias_rows")
+        nc.vector.memset(bias_rows[:], 0.0)
+        nc.scalar.dma_start(out=bias_rows[:M_TILES, :], in_=b.rearrange("(t m) o -> t (m o)", t=M_TILES))
+        identity = keep.tile([P, P], F32, name="identity")
+        make_identity(nc, identity[:])
+        bias_turned = psum.tile([P, P], F32, name="bias_turned", tag="bank7")
+        nc.tensor.transpose(bias_turned[:], bias_rows[:], identity[:])
+        bias = keep.tile([P, M_TILES], F32, name="bias")
+        nc.scalar.copy(out=bias[:], in_=bias_turned[:, :M_TILES])
 
         def load_words(g):
             window = keep.tile([P, T], I32, name="store_words%d" % g, align_bytes=64)
             nc.sync.dma_start(out=window[:], in_=s_words[g].rearrange("p c r -> p (c r)").bitcast(I32))
             return window
 
-        def load_rows(name, matrix, g, cols):
+        def load_rows(matrix, passes, cols):
             width = cols.stop - cols.start
-            raw = keep.tile([P, PACK, width], F32, name=name + "_raw")
-            rows = matrix[g * K_PASS : (g + 1) * K_PASS, cols]
-            nc.sync.dma_start(out=raw[:], in_=rows.rearrange("(p j) w -> p j w", j=PACK))
+            raw = stage.tile([P, len(passes), PACK, width], F32, name="raw", tag="raw")
+            for slot, g in enumerate(passes):
+                rows = matrix[g * K_PASS : (g + 1) * K_PASS, cols]
+                nc.sync.dma_start(out=raw[:, slot], in_=rows.rearrange("(p j) w -> p j w", j=PACK))
             return raw
 
         def interleave(name, raw, vector_cols):
@@ -108,9 +119,9 @@ def tile_picked_recall_bias_p_kernel(tc, xT, s_words, s_scales, w1, w2, b, offs,
             result = keep.tile([P, M_TILES, width], F32, name=name + "_result")
             for t in range(M_TILES):
                 if t in vector_tiles:
-                    nc.vector.tensor_scalar_add(result[:, t, :], banks[t][:], bias[:, t, :])
+                    nc.vector.tensor_scalar_add(result[:, t, :], banks[t][:], bias[:, t : t + 1])
                 else:
-                    nc.scalar.activation(out=result[:, t, :], in_=banks[t][:], func=IDENTITY, bias=bias[:, t, :])
+                    nc.scalar.activation(out=result[:, t, :], in_=banks[t][:], func=IDENTITY, bias=bias[:, t : t + 1])
                 if (t + 1) % tiles_per_store == 0:
                     ts = slice(t + 1 - tiles_per_store, t + 1)
                     nc.sync.dma_start(out=out_rows[:, ts, cols], in_=result[:, ts, :])
@@ -121,69 +132,71 @@ def tile_picked_recall_bias_p_kernel(tc, xT, s_words, s_scales, w1, w2, b, offs,
         c2 = slice(512, 768)
         c3 = slice(768, 1024)
 
+        w2_raw0 = load_rows(w2, [0], all_m)
         words0 = load_words(0)
-        nc.sync.dma_start(out=offsets[:], in_=offs)
-        w2_raw0 = load_rows("w2_0", w2, 0, all_m)
+        w2_raw1 = load_rows(w2, [1], all_m)
         words1 = load_words(1)
-        w2_raw1 = load_rows("w2_1", w2, 1, all_m)
-        w1_raw0 = load_rows("w1_0", w1, 0, all_m)
-        x0_raw0 = load_rows("x0_0", xT, 0, c0)
-        w1_raw1 = load_rows("w1_1", w1, 1, all_m)
-        x0_raw1 = load_rows("x0_1", xT, 1, c0)
-        x1_raw0 = load_rows("x1_0", xT, 0, c1)
-        x1_raw1 = load_rows("x1_1", xT, 1, c1)
-        x2_raw0 = load_rows("x2_0", xT, 0, c2)
-        x2_raw1 = load_rows("x2_1", xT, 1, c2)
-        x3_raw0 = load_rows("x3_0", xT, 0, c3)
-        x3_raw1 = load_rows("x3_1", xT, 1, c3)
+        w1_raw0 = load_rows(w1, [0], all_m)
 
+        w2_bf0 = interleave("w2_0", w2_raw0[:, 0], 0)
+        w1_raw1 = load_rows(w1, [1], all_m)
         picked0 = gather_words(0, words0)
-        w2_bf0 = interleave("w2_0", w2_raw0, 0)
+        w2_q0 = quantize("w2_0", w2_bf0)
         picked_scales = keep.tile([P, S], U8, name="picked_scales", align_bytes=64)
         nc.vector.tensor_copy(out=picked_scales[:], in_=store_scales[:].indirect(offsets[:]))
-        w2_q0 = quantize("w2_0", w2_bf0)
-        picked1 = gather_words(1, words1)
 
         banks0 = open_banks(0, 256)
         banks1 = open_banks(M_TILES, 256)
         one_pass(banks0, w2_q0, picked0[:, c0], picked_scales[:, c0], True, False)
         one_pass(banks1, w2_q0, picked0[:, c1], picked_scales[:, c1], True, False)
-        w2_q1 = quantize("w2_1", interleave("w2_1", w2_raw1, 128))
+        w2_bf1 = interleave("w2_1", w2_raw1[:, 0], 0)
+        x0_raw = load_rows(xT, [0, 1], c0)
+        picked1 = gather_words(1, words1)
+        w2_q1 = quantize("w2_1", w2_bf1)
         one_pass(banks0, w2_q1, picked1[:, c0], picked_scales[SCALE_ROWS:, c0], False, False)
         one_pass(banks1, w2_q1, picked1[:, c1], picked_scales[SCALE_ROWS:, c1], False, False)
-        w1_q0 = quantize("w1_0", interleave("w1_0", w1_raw0, 256))
+        w1_bf0 = interleave("w1_0", w1_raw0[:, 0], 256)
+        x1_raw = load_rows(xT, [0, 1], c1)
+        w1_q0 = quantize("w1_0", w1_bf0)
+        w1_bf1 = interleave("w1_1", w1_raw1[:, 0], 256)
+        x2_raw = load_rows(xT, [0, 1], c2)
 
-        x_bf = interleave("x0_0", x0_raw0, 128)
-        x_codes0, x_scales0 = quantize("x0_0", x_bf)
-        w1_q1 = quantize("w1_1", interleave("w1_1", w1_raw1, 256))
+        x_bf0 = interleave("x0_0", x0_raw[:, 0], 256)
+        w1_q1 = quantize("w1_1", w1_bf1)
+        x_codes0, x_scales0 = quantize("x0_0", x_bf0)
         one_pass(banks0, w1_q0, x_codes0[:], x_scales0[:], False, False)
-        x_codes1, x_scales1 = quantize("x0_1", interleave("x0_1", x0_raw1, 160))
+        x_bf1 = interleave("x0_1", x0_raw[:, 1], 128)
+        x3_raw = load_rows(xT, [0, 1], c3)
+        x_codes1, x_scales1 = quantize("x0_1", x_bf1)
         one_pass(banks0, w1_q1, x_codes1[:], x_scales1[:], False, True)
 
-        x_bf = interleave("x1_0", x1_raw0, 192)
+        x_bf0 = interleave("x1_0", x1_raw[:, 0], 192)
         finish("c0", banks0, c0, (), 4)
-        x_codes0, x_scales0 = quantize("x1_0", x_bf)
+        x_codes0, x_scales0 = quantize("x1_0", x_bf0)
         one_pass(banks1, w1_q0, x_codes0[:], x_scales0[:], False, False)
-        x_codes1, x_scales1 = quantize("x1_1", interleave("x1_1", x1_raw1, 192))
+        x_bf1 = interleave("x1_1", x1_raw[:, 1], 192)
+        x_codes1, x_scales1 = quantize("x1_1", x_bf1)
         one_pass(banks1, w1_q1, x_codes1[:], x_scales1[:], False, True)
         banks2 = open_banks(0, 256)
         one_pass(banks2, w2_q0, picked0[:, c2], picked_scales[:, c2], True, False)
         one_pass(banks2, w2_q1, picked1[:, c2], picked_scales[SCALE_ROWS:, c2], False, False)
 
-        x_bf = interleave("x2_0", x2_raw0, 192)
+        x_bf0 = interleave("x2_0", x2_raw[:, 0], 192)
         finish("c1", banks1, c1, (), 4)
-        x_codes0, x_scales0 = quantize("x2_0", x_bf)
+        x_codes0, x_scales0 = quantize("x2_0", x_bf0)
         one_pass(banks2, w1_q0, x_codes0[:], x_scales0[:], False, False)
-        x_codes1, x_scales1 = quantize("x2_1", interleave("x2_1", x2_raw1, 192))
+        x_bf1 = interleave("x2_1", x2_raw[:, 1], 192)
+        x_codes1, x_scales1 = quantize("x2_1", x_bf1)
         one_pass(banks2, w1_q1, x_codes1[:], x_scales1[:], False, True)
         banks3 = open_banks(4, 256)
         one_pass(banks3, w2_q0, picked0[:, c3], picked_scales[:, c3], True, False)
         one_pass(banks3, w2_q1, picked1[:, c3], picked_scales[SCALE_ROWS:, c3], False, False)
 
-        x_bf = interleave("x3_0", x3_raw0, 192)
+        x_bf0 = interleave("x3_0", x3_raw[:, 0], 192)
         finish("c2", banks2, c2, (), 4)
-        x_codes0, x_scales0 = quantize("x3_0", x_bf)
+        x_codes0, x_scales0 = quantize("x3_0", x_bf0)
         one_pass(banks3, w1_q0, x_codes0[:], x_scales0[:], False, False)
-        x_codes1, x_scales1 = quantize("x3_1", interleave("x3_1", x3_raw1, 168))
+        x_bf1 = interleave("x3_1", x3_raw[:, 1], 168)
+        x_codes1, x_scales1 = quantize("x3_1", x_bf1)
         one_pass(banks3, w1_q1, x_codes1[:], x_scales1[:], False, True)
         finish("c3", banks3, c3, (1, 3,), 2)

@@ -22,6 +22,7 @@ PASSES = K // K_PASS
 M_TILES = N // P
 QUADRANT = 32
 SCALE_ROWS = 4
+HALF = 512
 
 
 def tile_picked_recall_bias_p_kernel(tc, xT, s_words, s_scales, w1, w2, b, offs, out):
@@ -29,7 +30,7 @@ def tile_picked_recall_bias_p_kernel(tc, xT, s_words, s_scales, w1, w2, b, offs,
 
     with ExitStack() as ctx:
         keep = ctx.enter_context(tc.tile_pool(name="keep", bufs=1))
-        stage = ctx.enter_context(tc.tile_pool(name="stage", bufs=3))
+        stage = ctx.enter_context(tc.tile_pool(name="stage", bufs=5))
         psum = ctx.enter_context(tc.psum_pool(name="psum", bufs=1))
 
         offsets = keep.tile([P, S // 16], U16, name="offsets")
@@ -53,31 +54,36 @@ def tile_picked_recall_bias_p_kernel(tc, xT, s_words, s_scales, w1, w2, b, offs,
         nc.scalar.copy(out=bias[:], in_=bias_turned[:, :M_TILES])
 
         def load_words(g):
-            window = keep.tile([P, T], I32, name="store_words%d" % g, align_bytes=64)
+            window = stage.tile([P, T], I32, name="store_words", tag="staged")
             nc.sync.dma_start(out=window[:], in_=s_words[g].rearrange("p c r -> p (c r)").bitcast(I32))
             return window
 
-        def load_rows(matrix, passes, cols):
-            width = cols.stop - cols.start
-            raw = stage.tile([P, len(passes), PACK, width], F32, name="raw", tag="raw")
-            for slot, g in enumerate(passes):
+        def load_rows(pieces):
+            total = sum(cols.stop - cols.start for matrix, g, cols in pieces)
+            raw = stage.tile([P, PACK * total], F32, name="raw", tag="staged")
+            views = []
+            at = 0
+            for matrix, g, cols in pieces:
+                size = PACK * (cols.stop - cols.start)
+                view = raw[:, at : at + size].rearrange("p (j w) -> p j w", j=PACK)
                 rows = matrix[g * K_PASS : (g + 1) * K_PASS, cols]
-                nc.sync.dma_start(out=raw[:, slot], in_=rows.rearrange("(p j) w -> p j w", j=PACK))
-            return raw
+                nc.sync.dma_start(out=view, in_=rows.rearrange("(p j) w -> p j w", j=PACK))
+                views.append(view)
+                at += size
+            return views
 
         def interleave(name, raw, vector_cols):
             width = raw.shape[2]
             grouped = keep.tile([P, width, PACK], BF16, name=name + "_bf16", align_bytes=64)
-            split = width - vector_cols
-            if split > 0:
-                nc.scalar.copy(
-                    out=grouped[:, :split, :].rearrange("p (c i) j -> p c j i", i=4),
-                    in_=raw[:, :, :split].rearrange("p j (c i) -> p c j i", i=4),
-                )
             if vector_cols > 0:
                 nc.vector.tensor_copy(
-                    out=grouped[:, split:, :].rearrange("p (c i) j -> p c j i", i=4),
-                    in_=raw[:, :, split:].rearrange("p j (c i) -> p c j i", i=4),
+                    out=grouped[:, :vector_cols, :].rearrange("p (c i) j -> p c j i", i=4),
+                    in_=raw[:, :, :vector_cols].rearrange("p j (c i) -> p c j i", i=4),
+                )
+            if vector_cols < width:
+                nc.scalar.copy(
+                    out=grouped[:, vector_cols:, :].rearrange("p (c i) j -> p c j i", i=4),
+                    in_=raw[:, :, vector_cols:].rearrange("p j (c i) -> p c j i", i=4),
                 )
             return grouped
 
@@ -90,113 +96,88 @@ def tile_picked_recall_bias_p_kernel(tc, xT, s_words, s_scales, w1, w2, b, offs,
             )
             return codes, scales
 
-        def gather_words(g, window):
-            picked = keep.tile([P, S], U32, name="picked_words%d" % g, align_bytes=64)
-            nc.vector.tensor_copy(out=picked[:], in_=window[:].bitcast(U32).indirect(offsets[:]))
+        def gather_words(g, window, h):
+            picked = keep.tile([P, HALF], U32, name="picked_words%d_%d" % (g, h), align_bytes=64)
+            entries = offsets[:, h * HALF // 16 : (h + 1) * HALF // 16]
+            nc.vector.tensor_copy(out=picked[:], in_=window[:].bitcast(U32).indirect(entries))
             return picked
 
-        def one_pass(banks, weights, codes, scales, start, stop):
-            w_codes, w_scales = weights
-            for t in range(M_TILES):
-                m = slice(t * P, (t + 1) * P)
-                nc.tensor.matmul_mx(
-                    out=banks[t][:],
-                    lhsT=w_codes[:, m].bitcast(FP8X4),
-                    lhsT_scale=w_scales[:, m],
-                    rhs=codes.bitcast(FP8X4),
-                    rhs_scale=scales,
-                    start=start,
-                    stop=stop,
-                )
+        banks = {}
 
-        def open_banks(first, width):
-            return [psum.tile([P, width], F32, name="bank%d" % (first + t), tag="bank%d" % (first + t)) for t in range(M_TILES)]
+        def multiply(t, h, weights, first_tile, moving, start=False, stop=False):
+            if start:
+                tag = "bank%d" % (2 * t + h)
+                banks[t, h] = psum.tile([P, HALF], F32, name=tag, tag=tag)
+            w_codes, w_scales = weights
+            m = slice((t - first_tile) * P, (t - first_tile + 1) * P)
+            nc.tensor.matmul_mx(
+                out=banks[t, h][:],
+                lhsT=w_codes[:, m].bitcast(FP8X4),
+                lhsT_scale=w_scales[:, m],
+                rhs=moving[0].bitcast(FP8X4),
+                rhs_scale=moving[1],
+                start=start,
+                stop=stop,
+            )
 
         out_rows = out.rearrange("(t p) c -> p t c", p=P)
 
-        def finish(name, banks, cols, vector_tiles, tiles_per_store):
-            width = cols.stop - cols.start
-            result = keep.tile([P, M_TILES, width], F32, name=name + "_result")
+        def finish(h, vector_tiles, tiles_per_store):
+            result = keep.tile([P, M_TILES, HALF], F32, name="result%d" % h)
             for t in range(M_TILES):
                 if t in vector_tiles:
-                    nc.vector.tensor_scalar_add(result[:, t, :], banks[t][:], bias[:, t : t + 1])
+                    nc.vector.tensor_scalar_add(result[:, t, :], banks[t, h][:], bias[:, t : t + 1])
                 else:
-                    nc.scalar.activation(out=result[:, t, :], in_=banks[t][:], func=IDENTITY, bias=bias[:, t : t + 1])
+                    nc.scalar.activation(out=result[:, t, :], in_=banks[t, h][:], func=IDENTITY, bias=bias[:, t : t + 1])
                 if (t + 1) % tiles_per_store == 0:
                     ts = slice(t + 1 - tiles_per_store, t + 1)
-                    nc.sync.dma_start(out=out_rows[:, ts, cols], in_=result[:, ts, :])
+                    nc.sync.dma_start(out=out_rows[:, ts, halves[h]], in_=result[:, ts, :])
 
-        all_m = slice(0, N)
-        c0 = slice(0, 256)
-        c1 = slice(256, 512)
-        c2 = slice(512, 768)
-        c3 = slice(768, 1024)
+        all_m, all_j = slice(0, N), slice(0, S)
+        halves = (slice(0, HALF), slice(HALF, S))
 
-        w2_raw0 = load_rows(w2, [0], all_m)
+        (w2_raw0,) = load_rows([(w2, 0, all_m)])
         words0 = load_words(0)
-        w2_raw1 = load_rows(w2, [1], all_m)
+        (w2_raw1,) = load_rows([(w2, 1, all_m)])
         words1 = load_words(1)
-        w1_raw0 = load_rows(w1, [0], all_m)
 
-        w2_bf0 = interleave("w2_0", w2_raw0[:, 0], 0)
-        w1_raw1 = load_rows(w1, [1], all_m)
-        picked0 = gather_words(0, words0)
-        w2_q0 = quantize("w2_0", w2_bf0)
+        w2_bf0 = interleave("w2_0", w2_raw0, 0)
+        (w1_raw0,) = load_rows([(w1, 0, all_m)])
         picked_scales = keep.tile([P, S], U8, name="picked_scales", align_bytes=64)
         nc.vector.tensor_copy(out=picked_scales[:], in_=store_scales[:].indirect(offsets[:]))
+        picked0 = [gather_words(0, words0, h) for h in range(2)]
+        (x_raw0,) = load_rows([(xT, 0, all_j)])
+        w2_q0 = quantize("w2_0", w2_bf0)
+        for h in range(2):
+            for t in range(M_TILES):
+                multiply(t, h, w2_q0, 0, (picked0[h][:], picked_scales[:, halves[h]]), start=True)
 
-        banks0 = open_banks(0, 256)
-        banks1 = open_banks(M_TILES, 256)
-        one_pass(banks0, w2_q0, picked0[:, c0], picked_scales[:, c0], True, False)
-        one_pass(banks1, w2_q0, picked0[:, c1], picked_scales[:, c1], True, False)
-        w2_bf1 = interleave("w2_1", w2_raw1[:, 0], 0)
-        x0_raw = load_rows(xT, [0, 1], c0)
-        picked1 = gather_words(1, words1)
+        w2_bf1 = interleave("w2_1", w2_raw1, 0)
+        (w1_raw1,) = load_rows([(w1, 1, all_m)])
+        picked1 = [gather_words(1, words1, h) for h in range(2)]
+        x_raw1 = load_rows([(xT, 1, halves[0]), (xT, 1, halves[1])])
         w2_q1 = quantize("w2_1", w2_bf1)
-        one_pass(banks0, w2_q1, picked1[:, c0], picked_scales[SCALE_ROWS:, c0], False, False)
-        one_pass(banks1, w2_q1, picked1[:, c1], picked_scales[SCALE_ROWS:, c1], False, False)
-        w1_bf0 = interleave("w1_0", w1_raw0[:, 0], 256)
-        x1_raw = load_rows(xT, [0, 1], c1)
-        w1_q0 = quantize("w1_0", w1_bf0)
-        w1_bf1 = interleave("w1_1", w1_raw1[:, 0], 256)
-        x2_raw = load_rows(xT, [0, 1], c2)
+        for h in range(2):
+            for t in range(M_TILES):
+                multiply(t, h, w2_q1, 0, (picked1[h][:], picked_scales[SCALE_ROWS:, halves[h]]))
 
-        x_bf0 = interleave("x0_0", x0_raw[:, 0], 256)
+        w1_q0 = quantize("w1_0", interleave("w1_0", w1_raw0, 0))
+        x_bf0 = [interleave("x0_%d" % h, x_raw0[:, :, halves[h]], (512, 0)[h]) for h in range(2)]
+        codes, scales = quantize("x0_0", x_bf0[0])
+        for t in range(M_TILES):
+            multiply(t, 0, w1_q0, 0, (codes[:], scales[:]))
+        w1_bf1 = interleave("w1_1", w1_raw1, 256)
+        codes, scales = quantize("x0_1", x_bf0[1])
+        for t in range(M_TILES):
+            multiply(t, 1, w1_q0, 0, (codes[:], scales[:]))
         w1_q1 = quantize("w1_1", w1_bf1)
-        x_codes0, x_scales0 = quantize("x0_0", x_bf0)
-        one_pass(banks0, w1_q0, x_codes0[:], x_scales0[:], False, False)
-        x_bf1 = interleave("x0_1", x0_raw[:, 1], 128)
-        x3_raw = load_rows(xT, [0, 1], c3)
-        x_codes1, x_scales1 = quantize("x0_1", x_bf1)
-        one_pass(banks0, w1_q1, x_codes1[:], x_scales1[:], False, True)
 
-        x_bf0 = interleave("x1_0", x1_raw[:, 0], 192)
-        finish("c0", banks0, c0, (), 4)
-        x_codes0, x_scales0 = quantize("x1_0", x_bf0)
-        one_pass(banks1, w1_q0, x_codes0[:], x_scales0[:], False, False)
-        x_bf1 = interleave("x1_1", x1_raw[:, 1], 192)
-        x_codes1, x_scales1 = quantize("x1_1", x_bf1)
-        one_pass(banks1, w1_q1, x_codes1[:], x_scales1[:], False, True)
-        banks2 = open_banks(0, 256)
-        one_pass(banks2, w2_q0, picked0[:, c2], picked_scales[:, c2], True, False)
-        one_pass(banks2, w2_q1, picked1[:, c2], picked_scales[SCALE_ROWS:, c2], False, False)
-
-        x_bf0 = interleave("x2_0", x2_raw[:, 0], 192)
-        finish("c1", banks1, c1, (), 4)
-        x_codes0, x_scales0 = quantize("x2_0", x_bf0)
-        one_pass(banks2, w1_q0, x_codes0[:], x_scales0[:], False, False)
-        x_bf1 = interleave("x2_1", x2_raw[:, 1], 192)
-        x_codes1, x_scales1 = quantize("x2_1", x_bf1)
-        one_pass(banks2, w1_q1, x_codes1[:], x_scales1[:], False, True)
-        banks3 = open_banks(4, 256)
-        one_pass(banks3, w2_q0, picked0[:, c3], picked_scales[:, c3], True, False)
-        one_pass(banks3, w2_q1, picked1[:, c3], picked_scales[SCALE_ROWS:, c3], False, False)
-
-        x_bf0 = interleave("x3_0", x3_raw[:, 0], 192)
-        finish("c2", banks2, c2, (), 4)
-        x_codes0, x_scales0 = quantize("x3_0", x_bf0)
-        one_pass(banks3, w1_q0, x_codes0[:], x_scales0[:], False, False)
-        x_bf1 = interleave("x3_1", x3_raw[:, 1], 168)
-        x_codes1, x_scales1 = quantize("x3_1", x_bf1)
-        one_pass(banks3, w1_q1, x_codes1[:], x_scales1[:], False, True)
-        finish("c3", banks3, c3, (1, 3,), 2)
+        codes, scales = quantize("x1_0", interleave("x1_0", x_raw1[0], 320))
+        for t in range(M_TILES):
+            multiply(t, 0, w1_q1, 0, (codes[:], scales[:]), stop=True)
+        x_bf1 = interleave("x1_1", x_raw1[1], 512)
+        finish(0, (), 1)
+        codes, scales = quantize("x1_1", x_bf1)
+        for t in range(M_TILES):
+            multiply(t, 1, w1_q1, 0, (codes[:], scales[:]), stop=True)
+        finish(1, (1, 3), 1)

@@ -22,7 +22,6 @@ PASSES = K // K_PASS
 M_TILES = N // P
 QUADRANT = 32
 SCALE_ROWS = 4
-HALF = 512
 
 
 def tile_picked_recall_bias_p_kernel(tc, xT, s_words, s_scales, w1, w2, b, offs, out):
@@ -96,88 +95,94 @@ def tile_picked_recall_bias_p_kernel(tc, xT, s_words, s_scales, w1, w2, b, offs,
             )
             return codes, scales
 
-        def gather_words(g, window, h):
-            picked = keep.tile([P, HALF], U32, name="picked_words%d_%d" % (g, h), align_bytes=64)
-            entries = offsets[:, h * HALF // 16 : (h + 1) * HALF // 16]
-            nc.vector.tensor_copy(out=picked[:], in_=window[:].bitcast(U32).indirect(entries))
+        def gather_words(g, window):
+            picked = keep.tile([P, S], U32, name="picked_words%d" % g, align_bytes=64)
+            nc.vector.tensor_copy(out=picked[:], in_=window[:].bitcast(U32).indirect(offsets[:]))
             return picked
 
-        banks = {}
+        def open_banks(first, width):
+            tags = ["bank%d" % (first + t) for t in range(M_TILES)]
+            return [psum.tile([P, width], F32, name=tag, tag=tag) for tag in tags]
 
-        def multiply(t, h, weights, first_tile, moving, start=False, stop=False):
-            if start:
-                tag = "bank%d" % (2 * t + h)
-                banks[t, h] = psum.tile([P, HALF], F32, name=tag, tag=tag)
+        def one_pass(banks, weights, codes, scales, start=False, stop=False):
             w_codes, w_scales = weights
-            m = slice((t - first_tile) * P, (t - first_tile + 1) * P)
-            nc.tensor.matmul_mx(
-                out=banks[t, h][:],
-                lhsT=w_codes[:, m].bitcast(FP8X4),
-                lhsT_scale=w_scales[:, m],
-                rhs=moving[0].bitcast(FP8X4),
-                rhs_scale=moving[1],
-                start=start,
-                stop=stop,
-            )
+            for t in range(M_TILES):
+                m = slice(t * P, (t + 1) * P)
+                nc.tensor.matmul_mx(
+                    out=banks[t][:],
+                    lhsT=w_codes[:, m].bitcast(FP8X4),
+                    lhsT_scale=w_scales[:, m],
+                    rhs=codes.bitcast(FP8X4),
+                    rhs_scale=scales,
+                    start=start,
+                    stop=stop,
+                )
 
         out_rows = out.rearrange("(t p) c -> p t c", p=P)
 
-        def finish(h, vector_tiles, tiles_per_store):
-            result = keep.tile([P, M_TILES, HALF], F32, name="result%d" % h)
+        def finish(name, banks, cols, vector_tiles, tiles_per_store):
+            result = keep.tile([P, M_TILES, cols.stop - cols.start], F32, name=name + "_result")
             for t in range(M_TILES):
                 if t in vector_tiles:
-                    nc.vector.tensor_scalar_add(result[:, t, :], banks[t, h][:], bias[:, t : t + 1])
+                    nc.vector.tensor_scalar_add(result[:, t, :], banks[t][:], bias[:, t : t + 1])
                 else:
-                    nc.scalar.activation(out=result[:, t, :], in_=banks[t, h][:], func=IDENTITY, bias=bias[:, t : t + 1])
+                    nc.scalar.activation(out=result[:, t, :], in_=banks[t][:], func=IDENTITY, bias=bias[:, t : t + 1])
                 if (t + 1) % tiles_per_store == 0:
                     ts = slice(t + 1 - tiles_per_store, t + 1)
-                    nc.sync.dma_start(out=out_rows[:, ts, halves[h]], in_=result[:, ts, :])
+                    nc.sync.dma_start(out=out_rows[:, ts, cols], in_=result[:, ts, :])
 
-        all_m, all_j = slice(0, N), slice(0, S)
-        halves = (slice(0, HALF), slice(HALF, S))
+        all_m = slice(0, N)
+        wide, mid, last = slice(0, 512), slice(512, 768), slice(768, 1024)
 
-        (w2_raw0,) = load_rows([(w2, 0, all_m)])
         words0 = load_words(0)
-        (w2_raw1,) = load_rows([(w2, 1, all_m)])
+        (w2_raw0,) = load_rows([(w2, 0, all_m)])
         words1 = load_words(1)
-
-        w2_bf0 = interleave("w2_0", w2_raw0, 0)
+        (w2_raw1,) = load_rows([(w2, 1, all_m)])
         (w1_raw0,) = load_rows([(w1, 0, all_m)])
+
+        picked0 = gather_words(0, words0)
+        (wide_raw0,) = load_rows([(xT, 0, wide)])
         picked_scales = keep.tile([P, S], U8, name="picked_scales", align_bytes=64)
         nc.vector.tensor_copy(out=picked_scales[:], in_=store_scales[:].indirect(offsets[:]))
-        picked0 = [gather_words(0, words0, h) for h in range(2)]
-        (x_raw0,) = load_rows([(xT, 0, all_j)])
-        w2_q0 = quantize("w2_0", w2_bf0)
-        for h in range(2):
-            for t in range(M_TILES):
-                multiply(t, h, w2_q0, 0, (picked0[h][:], picked_scales[:, halves[h]]), start=True)
-
-        w2_bf1 = interleave("w2_1", w2_raw1, 0)
+        w2_bf0 = interleave("w2_0", w2_raw0, 0)
         (w1_raw1,) = load_rows([(w1, 1, all_m)])
-        picked1 = [gather_words(1, words1, h) for h in range(2)]
-        x_raw1 = load_rows([(xT, 1, halves[0]), (xT, 1, halves[1])])
+        w2_q0 = quantize("w2_0", w2_bf0)
+        wide_banks = open_banks(0, 512)
+        mid_banks = open_banks(M_TILES, 256)
+        one_pass(wide_banks, w2_q0, picked0[:, wide], picked_scales[:, wide], start=True)
+        one_pass(mid_banks, w2_q0, picked0[:, mid], picked_scales[:, mid], start=True)
+
+        picked1 = gather_words(1, words1)
+        (wide_raw1,) = load_rows([(xT, 1, wide)])
+        w2_bf1 = interleave("w2_1", w2_raw1, 128)
+        mid_raw0, mid_raw1 = load_rows([(xT, 0, mid), (xT, 1, mid)])
         w2_q1 = quantize("w2_1", w2_bf1)
-        for h in range(2):
-            for t in range(M_TILES):
-                multiply(t, h, w2_q1, 0, (picked1[h][:], picked_scales[SCALE_ROWS:, halves[h]]))
+        one_pass(wide_banks, w2_q1, picked1[:, wide], picked_scales[SCALE_ROWS:, wide])
+        one_pass(mid_banks, w2_q1, picked1[:, mid], picked_scales[SCALE_ROWS:, mid])
 
-        w1_q0 = quantize("w1_0", interleave("w1_0", w1_raw0, 0))
-        x_bf0 = [interleave("x0_%d" % h, x_raw0[:, :, halves[h]], (512, 0)[h]) for h in range(2)]
-        codes, scales = quantize("x0_0", x_bf0[0])
-        for t in range(M_TILES):
-            multiply(t, 0, w1_q0, 0, (codes[:], scales[:]))
-        w1_bf1 = interleave("w1_1", w1_raw1, 256)
-        codes, scales = quantize("x0_1", x_bf0[1])
-        for t in range(M_TILES):
-            multiply(t, 1, w1_q0, 0, (codes[:], scales[:]))
-        w1_q1 = quantize("w1_1", w1_bf1)
+        w1_bf0 = interleave("w1_0", w1_raw0, 192)
+        last_raw0, last_raw1 = load_rows([(xT, 0, last), (xT, 1, last)])
+        w1_q0 = quantize("w1_0", w1_bf0)
+        codes, scales = quantize("wide0", interleave("wide0", wide_raw0, 224))
+        one_pass(wide_banks, w1_q0, codes[:], scales[:])
+        w1_q1 = quantize("w1_1", interleave("w1_1", w1_raw1, 224))
+        codes, scales = quantize("wide1", interleave("wide1", wide_raw1, 320))
+        one_pass(wide_banks, w1_q1, codes[:], scales[:], stop=True)
 
-        codes, scales = quantize("x1_0", interleave("x1_0", x_raw1[0], 320))
-        for t in range(M_TILES):
-            multiply(t, 0, w1_q1, 0, (codes[:], scales[:]), stop=True)
-        x_bf1 = interleave("x1_1", x_raw1[1], 512)
-        finish(0, (), 1)
-        codes, scales = quantize("x1_1", x_bf1)
-        for t in range(M_TILES):
-            multiply(t, 1, w1_q1, 0, (codes[:], scales[:]), stop=True)
-        finish(1, (1, 3), 1)
+        mid_bf0 = interleave("mid0", mid_raw0, 96)
+        finish("wide", wide_banks, wide, (), 2)
+        codes, scales = quantize("mid0", mid_bf0)
+        one_pass(mid_banks, w1_q0, codes[:], scales[:])
+        codes, scales = quantize("mid1", interleave("mid1", mid_raw1, 256))
+        one_pass(mid_banks, w1_q1, codes[:], scales[:], stop=True)
+
+        last_banks = open_banks(0, 256)
+        one_pass(last_banks, w2_q0, picked0[:, last], picked_scales[:, last], start=True)
+        one_pass(last_banks, w2_q1, picked1[:, last], picked_scales[SCALE_ROWS:, last])
+        last_bf0 = interleave("last0", last_raw0, 256)
+        finish("mid", mid_banks, mid, (), 2)
+        codes, scales = quantize("last0", last_bf0)
+        one_pass(last_banks, w1_q0, codes[:], scales[:])
+        codes, scales = quantize("last1", interleave("last1", last_raw1, 256))
+        one_pass(last_banks, w1_q1, codes[:], scales[:], stop=True)
+        finish("last", last_banks, last, (1, 3), 2)

@@ -37,7 +37,7 @@ def tile_picked_recall_bias_p_kernel(tc, xT, s_words, s_scales, w1, w2, b, offs,
         store_scales = keep.tile([P, T], U8, name="store_scales", align_bytes=64)
         nc.vector.memset(store_scales[:].bitcast(I32), 0)
         for q in range(P // QUADRANT):
-            nc.scalar.dma_start(
+            nc.gpsimd.dma_start(
                 out=store_scales[QUADRANT * q : QUADRANT * q + PASSES * SCALE_ROWS, :].bitcast(I32),
                 in_=s_scales[:, SCALE_ROWS * q : SCALE_ROWS * (q + 1), :].bitcast(I32),
             )
@@ -154,7 +154,7 @@ def tile_picked_recall_bias_p_kernel(tc, xT, s_words, s_scales, w1, w2, b, offs,
 
         picked1 = gather_words(1, words1)
         (wide_raw1,) = load_rows([(xT, 1, wide)])
-        w2_bf1 = interleave("w2_1", w2_raw1, 128)
+        w2_bf1 = interleave("w2_1", w2_raw1, 0)
         mid_raw0, mid_raw1 = load_rows([(xT, 0, mid), (xT, 1, mid)])
         w2_q1 = quantize("w2_1", w2_bf1)
         one_pass(wide_banks, w2_q1, picked1[:, wide], picked_scales[SCALE_ROWS:, wide])

from contextlib import ExitStack

import concourse.mybir as mybir
from concourse.masks import make_identity

K, T, S, N = 1024, 2048, 1024, 512
FLOPS = 2 * 2 * K * N * S

F32 = mybir.dt.float32
BF16 = mybir.dt.bfloat16
I32 = mybir.dt.int32
U32 = mybir.dt.uint32
U16 = mybir.dt.uint16
U8 = mybir.dt.uint8
FP8X4 = mybir.dt.float8_e4m3fn_x4
IDENTITY = mybir.ActivationFunctionType.Identity

P = 128
PACK = 4
K_PASS = P * PACK
PASSES = K // K_PASS
M_TILES = N // P
QUADRANT = 32
SCALE_ROWS = 4


def tile_picked_recall_bias_p_kernel(tc, xT, s_words, s_scales, w1, w2, b, offs, out):
    nc = tc.nc

    with ExitStack() as ctx:
        keep = ctx.enter_context(tc.tile_pool(name="keep", bufs=1))
        stage = ctx.enter_context(tc.tile_pool(name="stage", bufs=5))
        psum = ctx.enter_context(tc.psum_pool(name="psum", bufs=1))

        offsets = keep.tile([P, S // 16], U16, name="offsets")
        nc.sync.dma_start(out=offsets[:], in_=offs)
        store_scales = keep.tile([P, T], U8, name="store_scales", align_bytes=64)
        nc.vector.memset(store_scales[:].bitcast(I32), 0)
        for q in range(P // QUADRANT):
            nc.gpsimd.dma_start(
                out=store_scales[QUADRANT * q : QUADRANT * q + PASSES * SCALE_ROWS, :].bitcast(I32),
                in_=s_scales[:, SCALE_ROWS * q : SCALE_ROWS * (q + 1), :].bitcast(I32),
            )

        bias_rows = keep.tile([P, P], F32, name="bias_rows")
        nc.vector.memset(bias_rows[:], 0.0)
        nc.scalar.dma_start(out=bias_rows[:M_TILES, :], in_=b.rearrange("(t m) o -> t (m o)", t=M_TILES))
        identity = keep.tile([P, P], F32, name="identity")
        make_identity(nc, identity[:])
        bias_turned = psum.tile([P, P], F32, name="bias_turned", tag="bank7")
        nc.tensor.transpose(bias_turned[:], bias_rows[:], identity[:])
        bias = keep.tile([P, M_TILES], F32, name="bias")
        nc.scalar.copy(out=bias[:], in_=bias_turned[:, :M_TILES])

        def load_words(g):
            window = stage.tile([P, T], I32, name="store_words", tag="staged")
            nc.sync.dma_start(out=window[:], in_=s_words[g].rearrange("p c r -> p (c r)").bitcast(I32))
            return window

        def load_rows(pieces):
            total = sum(cols.stop - cols.start for matrix, g, cols in pieces)
            raw = stage.tile([P, PACK * total], F32, name="raw", tag="staged")
            views = []
            at = 0
            for matrix, g, cols in pieces:
                size = PACK * (cols.stop - cols.start)
                view = raw[:, at : at + size].rearrange("p (j w) -> p j w", j=PACK)
                rows = matrix[g * K_PASS : (g + 1) * K_PASS, cols]
                nc.sync.dma_start(out=view, in_=rows.rearrange("(p j) w -> p j w", j=PACK))
                views.append(view)
                at += size
            return views

        def interleave(name, raw, vector_cols):
            width = raw.shape[2]
            grouped = keep.tile([P, width, PACK], BF16, name=name + "_bf16", align_bytes=64)
            if vector_cols > 0:
                nc.vector.tensor_copy(
                    out=grouped[:, :vector_cols, :].rearrange("p (c i) j -> p c j i", i=4),
                    in_=raw[:, :, :vector_cols].rearrange("p j (c i) -> p c j i", i=4),
                )
            if vector_cols < width:
                nc.scalar.copy(
                    out=grouped[:, vector_cols:, :].rearrange("p (c i) j -> p c j i", i=4),
                    in_=raw[:, :, vector_cols:].rearrange("p j (c i) -> p c j i", i=4),
                )
            return grouped

        def quantize(name, grouped):
            width = grouped.shape[1]
            codes = keep.tile([P, width], U32, name=name + "_codes", align_bytes=64)
            scales = keep.tile([P, width], U8, name=name + "_scales", align_bytes=64)
            nc.vector.quantize_mx(
                out=codes[:].bitcast(FP8X4), scales=scales[:], in_=grouped[:].rearrange("p w j -> p (w j)")
            )
            return codes, scales

        def gather_words(g, window):
            picked = keep.tile([P, S], U32, name="picked_words%d" % g, align_bytes=64)
            nc.vector.tensor_copy(out=picked[:], in_=window[:].bitcast(U32).indirect(offsets[:]))
            return picked

        def open_banks(first, width):
            tags = ["bank%d" % (first + t) for t in range(M_TILES)]
            return [psum.tile([P, width], F32, name=tag, tag=tag) for tag in tags]

        def one_pass(banks, weights, codes, scales, start=False, stop=False):
            w_codes, w_scales = weights
            for t in range(M_TILES):
                m = slice(t * P, (t + 1) * P)
                nc.tensor.matmul_mx(
                    out=banks[t][:],
                    lhsT=w_codes[:, m].bitcast(FP8X4),
                    lhsT_scale=w_scales[:, m],
                    rhs=codes.bitcast(FP8X4),
                    rhs_scale=scales,
                    start=start,
                    stop=stop,
                )

        out_rows = out.rearrange("(t p) c -> p t c", p=P)

        def finish(name, banks, cols, vector_tiles, tiles_per_store):
            result = keep.tile([P, M_TILES, cols.stop - cols.start], F32, name=name + "_result")
            for t in range(M_TILES):
                if t in vector_tiles:
                    nc.vector.tensor_scalar_add(result[:, t, :], banks[t][:], bias[:, t : t + 1])
                else:
                    nc.scalar.activation(out=result[:, t, :], in_=banks[t][:], func=IDENTITY, bias=bias[:, t : t + 1])
                if (t + 1) % tiles_per_store == 0:
                    ts = slice(t + 1 - tiles_per_store, t + 1)
                    nc.sync.dma_start(out=out_rows[:, ts, cols], in_=result[:, ts, :])

        all_m = slice(0, N)
        wide, mid, last = slice(0, 512), slice(512, 768), slice(768, 1024)

        words0 = load_words(0)
        (w2_raw0,) = load_rows([(w2, 0, all_m)])
        words1 = load_words(1)
        (w2_raw1,) = load_rows([(w2, 1, all_m)])
        (w1_raw0,) = load_rows([(w1, 0, all_m)])

        picked0 = gather_words(0, words0)
        (wide_raw0,) = load_rows([(xT, 0, wide)])
        picked_scales = keep.tile([P, S], U8, name="picked_scales", align_bytes=64)
        nc.vector.tensor_copy(out=picked_scales[:], in_=store_scales[:].indirect(offsets[:]))
        w2_bf0 = interleave("w2_0", w2_raw0, 0)
        (w1_raw1,) = load_rows([(w1, 1, all_m)])
        w2_q0 = quantize("w2_0", w2_bf0)
        wide_banks = open_banks(0, 512)
        mid_banks = open_banks(M_TILES, 256)
        one_pass(wide_banks, w2_q0, picked0[:, wide], picked_scales[:, wide], start=True)
        one_pass(mid_banks, w2_q0, picked0[:, mid], picked_scales[:, mid], start=True)

        picked1 = gather_words(1, words1)
        (wide_raw1,) = load_rows([(xT, 1, wide)])
        w2_bf1 = interleave("w2_1", w2_raw1, 0)
        mid_raw0, mid_raw1 = load_rows([(xT, 0, mid), (xT, 1, mid)])
        w2_q1 = quantize("w2_1", w2_bf1)
        one_pass(wide_banks, w2_q1, picked1[:, wide], picked_scales[SCALE_ROWS:, wide])
        one_pass(mid_banks, w2_q1, picked1[:, mid], picked_scales[SCALE_ROWS:, mid])

        w1_bf0 = interleave("w1_0", w1_raw0, 192)
        last_raw0, last_raw1 = load_rows([(xT, 0, last), (xT, 1, last)])
        w1_q0 = quantize("w1_0", w1_bf0)
        codes, scales = quantize("wide0", interleave("wide0", wide_raw0, 224))
        one_pass(wide_banks, w1_q0, codes[:], scales[:])
        w1_q1 = quantize("w1_1", interleave("w1_1", w1_raw1, 224))
        codes, scales = quantize("wide1", interleave("wide1", wide_raw1, 320))
        one_pass(wide_banks, w1_q1, codes[:], scales[:], stop=True)

        mid_bf0 = interleave("mid0", mid_raw0, 96)
        finish("wide", wide_banks, wide, (), 2)
        codes, scales = quantize("mid0", mid_bf0)
        one_pass(mid_banks, w1_q0, codes[:], scales[:])
        codes, scales = quantize("mid1", interleave("mid1", mid_raw1, 256))
        one_pass(mid_banks, w1_q1, codes[:], scales[:], stop=True)

        last_banks = open_banks(0, 256)
        one_pass(last_banks, w2_q0, picked0[:, last], picked_scales[:, last], start=True)
        one_pass(last_banks, w2_q1, picked1[:, last], picked_scales[SCALE_ROWS:, last])
        last_bf0 = interleave("last0", last_raw0, 256)
        finish("mid", mid_banks, mid, (), 2)
        codes, scales = quantize("last0", last_bf0)
        one_pass(last_banks, w1_q0, codes[:], scales[:])
        codes, scales = quantize("last1", interleave("last1", last_raw1, 256))
        one_pass(last_banks, w1_q1, codes[:], scales[:], stop=True)
        finish("last", last_banks, last, (1, 3), 2)
